import numpy as np
import ml_dtypes


def mxq(x, axis, fmt="e4m3"):
    dtype, down = {"e4m3": (ml_dtypes.float8_e4m3fn, 7), "e5m2": (ml_dtypes.float8_e5m2, 14)}[fmt]
    v = np.moveaxis(np.asarray(x, np.float32).astype(ml_dtypes.bfloat16).astype(np.float64), axis, -1)
    blocks = v.reshape(v.shape[:-1] + (-1, 32))
    amax = np.abs(blocks).max(-1, keepdims=True)
    byte = np.maximum(np.where(amax > 0, np.frexp(amax)[1] - 1 + 127, 0) - down, 1)
    scale = np.exp2(byte - 127.0)
    codes = (blocks / scale).astype(np.float32).astype(dtype).astype(np.float64)
    return np.moveaxis((codes * scale).reshape(v.shape), -1, axis)


WIDE = False


def mx_kscale(k):
    if not WIDE:
        return np.ones(k)
    levels = np.array([10, -10, 5, -5, 0])
    if k % 512:
        return np.exp2(np.random.permutation(np.resize(levels, k // 32))).repeat(32)
    a = np.empty((k // 512, 16))
    for p in range(k // 512):
        a[p, :8] = np.random.permutation(np.resize(levels, 8))
        for g in range(8):
            far = levels[np.abs(levels - a[p, g]) >= 10]
            a[p, g + 8] = far[np.random.randint(len(far))]
    return np.exp2(a.ravel()).repeat(32)


def f64(x):
    return np.asarray(x).astype(np.float64)


def striped(idx):
    return np.tile(idx.reshape(-1, 16).T, (8, 1)).astype(np.uint16)


def unstriped(offs):
    return offs[:16].T.reshape(-1).astype(np.int64)


E2M1 = np.array([0.0, 0.5, 1.0, 1.5, 2.0, 3.0, 4.0, 6.0, -0.0, -0.5, -1.0, -1.5, -2.0, -3.0, -4.0, -6.0])


def pack_weight(w, fmt):
    k, n = w.shape
    w = f64(np.asarray(w, np.float32).astype(ml_dtypes.bfloat16)).reshape(k // 32, 32, n)
    amax = np.abs(w).max(1)
    if fmt == "e4m3":
        byte = np.frexp(amax)[1] - 1 + 127 - 7
    else:
        mant, ex = np.frexp(amax / 6.0)
        byte = np.where(mant > 0.5, ex, ex - 1) + 127
    byte = np.clip(np.where(amax > 0, byte, 1), 1, 254)
    scaled = (w * np.exp2(127.0 - byte)[:, None, :]).reshape(k, n).astype(np.float32)
    by_word = np.ascontiguousarray(scaled.reshape(k // 512, 128, 4, n).transpose(0, 1, 3, 2))
    if fmt == "e4m3":
        words = by_word.astype(ml_dtypes.float8_e4m3fn).view(np.uint8)
    else:
        c = by_word.astype(ml_dtypes.float4_e2m1fn).view(np.uint8) & 0xF
        words = (c[..., 0::2] | (c[..., 1::2] << 4)).reshape(k // 512, 128, 2 * n)
    return np.ascontiguousarray(words), np.ascontiguousarray(byte.astype(np.uint8).reshape(k // 512, 16, n))


def unpack_weight(words, scales, fmt):
    g, _, n = scales.shape
    words = np.ascontiguousarray(words).reshape(g, 128, n, -1)
    if fmt == "e4m3":
        vals = words.view(ml_dtypes.float8_e4m3fn).astype(np.float64)
    else:
        nib = np.empty((g, 128, n, 4), np.uint8)
        nib[..., 0::2] = words & 0xF
        nib[..., 1::2] = words >> 4
        vals = E2M1[nib]
    vals = vals * np.repeat(np.exp2(scales.astype(np.float64) - 127.0), 8, axis=1)[..., None]
    return vals.transpose(0, 1, 3, 2).reshape(g * 512, n)


def gelu(v):
    return 0.5 * v * (1.0 + np.tanh(np.sqrt(2.0 / np.pi) * (v + 0.044715 * v**3)))


K, H, N, T, S = 1024, 1024, 512, 2048, 1024

def setup_inputs():
    n = np.random.standard_normal
    s = mx_kscale(K)[:, None]
    u = mx_kscale(H)[:, None]
    tab_words, tab_scales = pack_weight(n((K, T)) * s, "e4m3")
    w2_words, w2_scales = pack_weight(n((K, H)) / np.sqrt(K) / s * u.T, "e2m1")
    return {
        "tab_words": tab_words, "tab_scales": tab_scales,
        "offs": striped(np.random.permutation(T)[:S]),
        "w1": (n((K, H)) / np.sqrt(K) / s * u.T).astype(np.float32),
        "b1": (0.5 * n(H) * u[:, 0]).astype(np.float32),
        "w2_words": w2_words, "w2_scales": w2_scales,
        "b2": (0.5 * n(H) * u[:, 0]).astype(np.float32),
        "wc": (n((H, N)) / np.sqrt(H) / u).astype(np.float32),
        "bc": (0.5 * n(N)).astype(np.float32),
    }

def reference(tab_words, tab_scales, offs, w1, b1, w2_words, w2_scales, b2, wc, bc):
    v = unpack_weight(tab_words, tab_scales, "e4m3")[:, unstriped(offs)]
    w1q = mxq(f64(w1), 0, "e4m3")
    w2q = unpack_weight(w2_words, w2_scales, "e2m1")
    a = (w1q.T @ v) + f64(b1)[:, None]
    b = (w2q.T @ v) + f64(b2)[:, None]
    h = np.maximum(a, b)
    hq = mxq(h, 0, "e4m3")
    wcq = mxq(f64(wc), 0, "e4m3")
    return (wcq.T @ hq) + f64(bc)[:, None]

@@ -1,0 +1,314 @@
+from contextlib import ExitStack
+
+import concourse.mybir as mybir
+
+K, H, N, T, S = 1024, 1024, 512, 2048, 1024
+FLOPS = 2 * S * (2 * K * H + H * N)
+
+F32 = mybir.dt.float32
+BF16 = mybir.dt.bfloat16
+I32 = mybir.dt.int32
+U32 = mybir.dt.uint32
+U16 = mybir.dt.uint16
+U8 = mybir.dt.uint8
+FP8X4 = mybir.dt.float8_e4m3fn_x4
+FP4X4 = mybir.dt.float4_e2m1fn_x4
+ADD = mybir.AluOpType.add
+MULT = mybir.AluOpType.mult
+MAX = mybir.AluOpType.max
+IS_EQUAL = mybir.AluOpType.is_equal
+IDENT = mybir.ActivationFunctionType.Identity
+
+P = 128
+PASS = 512
+HALF = 512
+
+
+def move(nc, eng, out, in_):
+    if eng == "v":
+        nc.vector.tensor_copy(out=out, in_=in_)
+    elif eng == "s":
+        nc.scalar.copy(out=out, in_=in_)
+    else:
+        nc.gpsimd.tensor_scalar(out=out, in0=in_, scalar1=1.0, scalar2=0.0, op0=MULT, op1=ADD)
+
+
+def tile_list_patch_maxout_evidence_kernel(tc, tab_words, tab_scales, offs, w1, b1, w2_words, w2_scales, b2, wc, bc, out):
+    nc = tc.nc
+    with ExitStack() as ctx:
+        first = ctx.enter_context(tc.tile_pool(name="first", bufs=1))
+        psum = ctx.enter_context(tc.psum_pool(name="psum", bufs=1))
+
+        def bank(k, shape):
+            return psum.tile(shape, F32, name="bank%d" % k, tag="bank%d" % k)
+
+        offs_t = first.tile([P, S // 16], U16, name="offs_t")
+        nc.sync.dma_start(offs_t[:], offs)
+
+        rows_raw = first.tile([4, PASS], F32, name="rows_raw", align_bytes=64)
+        nc.sync.dma_start(out=rows_raw[0:2, :], in_=b1.rearrange("(b c) -> b c", b=2))
+        nc.sync.dma_start(out=rows_raw[2:4, :], in_=b2.rearrange("(b c) -> b c", b=2))
+
+        tsc = first.tile([P, 2, T // 4], I32, name="tsc", align_bytes=64)
+        w2s_raw = first.tile([P, 2, H // 4], I32, name="w2s_raw", tag="w2s_raw", align_bytes=64)
+        rows = first.tile([P, PASS], F32, name="rows", align_bytes=64)
+        rows_c = first.tile([P, P], F32, name="rows_c", align_bytes=64)
+        ident = first.tile([P, P], F32, name="ident", align_bytes=64)
+        nc.gpsimd.memset(tsc[:, 0, :], 0)
+        nc.vector.memset(tsc[:, 1, :], 0)
+        nc.vector.memset(w2s_raw[:], 0)
+        with tc.tile_pool(name="setup", bufs=1) as setup:
+            diag = setup.tile([P, P], I32, name="diag")
+            nc.gpsimd.iota(diag[:], pattern=[[-1, P]], base=0, channel_multiplier=1)
+            nc.vector.tensor_scalar(out=ident[:], in0=diag[:], scalar1=0.0, scalar2=None, op0=IS_EQUAL)
+        nc.vector.memset(rows[:], 0.0)
+        nc.vector.memset(rows_c[:], 0.0)
+        held = ctx.enter_context(tc.tile_pool(name="held", bufs=1))
+
+        def place(shape, dtype, name, size, over):
+            pool = first if over == "w2s_raw" else held
+            return pool.tile(shape, dtype, name=name, tag=over or name, align_bytes=64)
+
+        tsc_src = tab_scales.bitcast(I32).rearrange("a (q r) n -> r q a n", r=4)
+        for r in range(4):
+            nc.sync.dma_start(out=tsc[r:P:32, :, :], in_=tsc_src[r])
+        w2s_src = w2_scales.bitcast(I32).rearrange("a (q r) n -> r q a n", r=4)
+        tw = [place([P, T], I32, "tw%d" % a, 0, None) for a in range(2)]
+        w2w_raw = place([P, 2, H // 2], I32, "w2w_raw", 0, "w2w_raw")
+        w1_raw = {}
+        wc_raw = {}
+
+        def load_w1(a, b):
+            t_w = place([P, 4, PASS], F32, "w1raw%d%d" % (a, b), 0, "w%d%d" % (a, b))
+            nc.sync.dma_start(
+                out=t_w[:],
+                in_=w1[a * PASS:(a + 1) * PASS, b * PASS:(b + 1) * PASS].rearrange("(p j) c -> p j c", j=4),
+            )
+            w1_raw[a, b] = t_w
+
+        def load_wc(b):
+            t_w = place([P, 4, N], F32, "wcraw%d" % b, 0, "wc%d" % b)
+            src = wc[b * PASS:(b + 1) * PASS, :].rearrange("(g t i) n -> t g i n", t=4, i=4)
+            for t in range(4):
+                nc.sync.dma_start(out=t_w[:, t, :], in_=src[t])
+            wc_raw[b] = t_w
+
+        nc.sync.dma_start(out=tw[0][:], in_=tab_words[0].rearrange("p t i -> p (t i)").bitcast(I32))
+        nc.sync.dma_start(out=w2w_raw[:], in_=w2_words.bitcast(I32).rearrange("a p n -> p a n"))
+        for r in range(4):
+            nc.sync.dma_start(out=w2s_raw[r:P:32, :, :], in_=w2s_src[r])
+        nc.sync.dma_start(out=tw[1][:], in_=tab_words[1].rearrange("p t i -> p (t i)").bitcast(I32))
+        load_w1(1, 0)
+        load_w1(0, 0)
+        load_w1(0, 1)
+        load_w1(1, 1)
+        load_wc(1)
+        load_wc(0)
+
+        nc.sync.dma_start(out=rows_c[0:4, :], in_=bc.rearrange("(m p) -> m p", p=P))
+        bias_c = first.tile([P, 4], F32, name="bias_c")
+
+        def make_bias_c(k):
+            bias_c_ps = bank(k, [P, P])
+            nc.tensor.transpose(bias_c_ps[:], rows_c[:], ident[:])
+            nc.scalar.activation(out=bias_c[:], in_=bias_c_ps[:, 0:4], func=IDENT)
+
+        gw = {}
+        gs = {}
+        gs_b = {}
+
+        def gather_scales(a, c, over=None):
+            g = place([P, HALF], U8, "gs%d%d" % (a, c), 512, over)
+            nc.vector.tensor_copy(out=g[:], in_=tsc[:, a, :].bitcast(U8).indirect(offs_t[:, 32 * c:32 * (c + 1)]))
+            gs[a, c] = g[:]
+            gs_b[a, c] = g[:]
+
+        def gather_words(a, c, over=None):
+            g = place([P, HALF], U32, "gw%d%d" % (a, c), 2048, over)
+            nc.vector.tensor_copy(out=g[:], in_=tw[a][:].bitcast(U32).indirect(offs_t[:, 32 * c:32 * (c + 1)]))
+            gw[a, c] = g
+
+        w2w = held.tile([P, 4, 4, 64], I32, name="w2w", align_bytes=64)
+        w2s = held.tile([P, 4, 4, 32], I32, name="w2s", align_bytes=64)
+
+        def order_w2():
+            nc.vector.tensor_copy(
+                out=w2w[:].rearrange("p u t (g w) -> p u t g w", w=2),
+                in_=w2w_raw[:].rearrange("p a (b g t w) -> p (a b) t g w", b=2, t=4, w=2),
+            )
+            nc.vector.tensor_copy(
+                out=w2s[:].rearrange("p u t g -> p u g t"),
+                in_=w2s_raw[:].rearrange("p a (b g t) -> p (a b) g t", b=2, t=4),
+            )
+
+        bias = first.tile([P, 4, 4], F32, name="bias")
+
+        def make_bias():
+            nc.scalar.copy(
+                out=rows[0:4, :].rearrange("b (t g i) -> b t g i", t=4, i=4),
+                in_=rows_raw[:].rearrange("b (g t i) -> b t g i", t=4, i=4),
+            )
+            bias_ps = bank(7, [P, 4, P])
+            for t in range(4):
+                nc.tensor.transpose(bias_ps[:, t, :], rows[:, t * P:(t + 1) * P], ident[:])
+            nc.scalar.activation(out=bias[:], in_=bias_ps[:, :, 0:4], func=IDENT)
+
+        bb = {}
+
+        def branch_b(c, b, k0, over=None):
+            accs = [bank(k0 + t, [P, HALF]) for t in range(4)]
+            for a in range(2):
+                for t in range(4):
+                    nc.tensor.matmul_mx(
+                        out=accs[t][:],
+                        lhsT=w2w[:, 2 * a + b, t, :].bitcast(U8).bitcast(FP4X4),
+                        lhsT_scale=w2s[:, 2 * a + b, t, :].bitcast(U8),
+                        rhs=gw[a, c][:].bitcast(FP8X4),
+                        rhs_scale=gs_b[a, c],
+                        start=(a == 0),
+                        stop=(a == 1),
+                    )
+            v = place([P, 4, HALF], F32, "bb%d%d" % (c, b), 0, over)
+            for t in range(4):
+                nc.scalar.activation(out=v[:, t, :], in_=accs[t][:], func=IDENT, bias=bias[:, t, 2 + b:3 + b])
+                bb[c, b, t] = v[:, t, :]
+
+        def cast_w1(a, b, eng, g):
+            dst = g.rearrange("p (t g i j) -> p t g j i", t=4, i=4, j=4)
+            src = w1_raw[a, b][:].rearrange("p j (g t i) -> p t g j i", t=4, i=4)
+            if eng == "g":
+                for t in range(4):
+                    move(nc, eng, dst[:, t], src[:, t])
+            else:
+                move(nc, eng, dst, src)
+
+        def quant(name, g, width, over=None):
+            codes = place([P, width], U32, name + "c", 4 * width, over)
+            scales = held.tile([P, width], U8, name=name + "s", align_bytes=64)
+            nc.vector.quantize_mx(out=codes[:].bitcast(FP8X4), scales=scales[:], in_=g)
+            return codes, scales
+
+        def interleave(eng, g, raw):
+            dst = g.rearrange("p (c i t) -> p c t i", i=4, t=4)
+            src = raw.rearrange("p t (c i) -> p c t i", i=4)
+            parts = 4 if eng == "g" else 1
+            w = dst.shape[1] // parts
+            for u in range(parts):
+                move(nc, eng, dst[:, u * w:(u + 1) * w], src[:, u * w:(u + 1) * w])
+
+        w1q = {}
+        wcq = {}
+
+        def branch_a(c, b, k0):
+            accs = [bank(k0 + t, [P, HALF]) for t in range(4)]
+            for t in range(4):
+                for a in range(2):
+                    codes, scales = w1q[a, b]
+                    nc.tensor.matmul_mx(
+                        out=accs[t][:],
+                        lhsT=codes[:, t * P:(t + 1) * P].bitcast(FP8X4),
+                        lhsT_scale=scales[:, t * P:(t + 1) * P],
+                        rhs=gw[a, c][:].bitcast(FP8X4),
+                        rhs_scale=gs[a, c],
+                        start=(a == 0),
+                        stop=(a == 1),
+                    )
+            return accs
+
+        def maxout(accs, c, b, lo, width, over=None):
+            planes = place([P, 4, width], BF16, "planes%d%d%d" % (c, b, lo), 8 * width, over)
+            for t in range(4):
+                nc.vector.scalar_tensor_tensor(
+                    out=planes[:, t, :], in0=accs[t][:, lo:lo + width], scalar=bias[:, t, b:b + 1],
+                    in1=bb[c, b, t][:, lo:lo + width], op0=ADD, op1=MAX,
+                )
+            return planes[:]
+
+        def head(col, width, h0, lo0, h1, engs, banks):
+            per = 4 // len(banks)
+            tiles = [bank(k, [P, per, width]) for k in banks]
+            accs = [tiles[m // per][:, m % per, :] for m in range(4)]
+            order = [(b, m) for b in range(2) for m in range(4)] if per == 1 else [(b, m) for m in range(4) for b in range(2)]
+            for b, m in order:
+                codes, scales = wcq[b]
+                hc, hs = (h0, h1)[b]
+                lo = lo0 if b == 0 else 0
+                nc.tensor.matmul_mx(
+                    out=accs[m],
+                    lhsT=codes[:, m * P:(m + 1) * P].bitcast(FP8X4),
+                    lhsT_scale=scales[:, m * P:(m + 1) * P],
+                    rhs=hc[:, lo:lo + width].bitcast(FP8X4),
+                    rhs_scale=hs[:, lo:lo + width],
+                    start=(b == 0),
+                    stop=(b == 1),
+                )
+            dst = out.rearrange("(m p) n -> p m n", p=P)
+            per_store = 1 if width == HALF else 2
+            for m0 in range(0, 4, per_store):
+                res = held.tile([P, per_store, width], F32, name="res%d_%d" % (col, m0))
+                for m in range(m0, m0 + per_store):
+                    if engs[m] == "s":
+                        nc.scalar.activation(out=res[:, m - m0, :], in_=accs[m], func=IDENT, bias=bias_c[:, m:m + 1])
+                    else:
+                        nc.vector.tensor_scalar(out=res[:, m - m0, :], in0=accs[m], scalar1=bias_c[:, m:m + 1], scalar2=None, op0=ADD)
+                nc.sync.dma_start(out=dst[:, m0:m0 + per_store, col:col + width], in_=res[:])
+
+        make_bias()
+        w1bf = [place([P, 2, 4 * PASS], BF16, "w1bf%d" % b, 0, None) for b in range(2)]
+        wcbf = place([P, 2, 4 * N], BF16, "wcbf", 0, None)
+        gather_scales(0, 0)
+        gather_scales(1, 0)
+        gather_words(0, 0)
+        order_w2()
+        gather_scales(0, 1, "w2s_raw")
+        gather_words(1, 0)
+        branch_b(0, 0, 0)
+        branch_b(0, 1, 4)
+        gather_scales(1, 1, "w2w_raw")
+        gather_words(1, 1)
+        gather_words(0, 1, "tw1")
+        cast_w1(0, 1, "v", w1bf[1][:, 0, :])
+        cast_w1(1, 0, "v", w1bf[0][:, 1, :])
+        branch_b(1, 0, 0)
+        cast_w1(0, 0, "v", w1bf[0][:, 0, :])
+        cq, cs = quant("w1q0", w1bf[0][:].rearrange("p a n -> p (a n)"), 2 * PASS)
+        for a in range(2):
+            w1q[a, 0] = (cq[:, a * PASS:(a + 1) * PASS], cs[:, a * PASS:(a + 1) * PASS])
+        cast_w1(1, 1, "s", w1bf[1][:, 1, :])
+        a00 = branch_a(0, 0, 0)
+        interleave("v", wcbf[:, 1, :], wc_raw[1][:])
+        p00 = maxout(a00, 0, 0, 0, 512)
+        cq, cs = quant("w1q1", w1bf[1][:].rearrange("p a n -> p (a n)"), 2 * PASS, "w00")
+        for a in range(2):
+            w1q[a, 1] = (cq[:, a * PASS:(a + 1) * PASS], cs[:, a * PASS:(a + 1) * PASS])
+        branch_b(1, 1, 4, "bb00")
+        a01 = branch_a(0, 1, 0)
+        p01 = maxout(a01, 0, 1, 0, 512)
+        a10 = branch_a(1, 0, 4)
+        h00 = place([P, 2048], BF16, "h00", 0, None)
+        interleave("s", h00[:], p00)
+        q00 = quant("hq00", h00[:], 512, "wc1")
+        p10 = maxout(a10, 1, 0, 0, 512)
+        make_bias_c(3)
+        h10 = place([P, 2048], BF16, "h10", 0, "w10")
+        interleave("s", h10[:], p10)
+        a11 = branch_a(1, 1, 4)
+        interleave("s", wcbf[:, 0, :], wc_raw[0][:])
+        q10 = quant("hq10", h10[:], 512, "bb10")
+        cq, cs = quant("wcq", wcbf[:].rearrange("p b n -> p (b n)"), 2 * N)
+        for b in range(2):
+            wcq[b] = (cq[:, b * N:(b + 1) * N], cs[:, b * N:(b + 1) * N])
+        pl1 = maxout(a11, 1, 1, 256, 256)
+        h01 = place([P, 2048], BF16, "h01", 0, None)
+        interleave("s", h01[:], p01)
+        hl1 = place([P, 1024], BF16, "hl1", 0, None)
+        interleave("v", hl1[:], pl1)
+        q01 = quant("hq01", h01[:], 512)
+        pl0 = maxout(a11, 1, 1, 0, 256, "planes000")
+        hl0 = place([P, 1024], BF16, "hl0", 0, None)
+        interleave("v", hl0[:], pl0)
+        ql1 = quant("hql1", hl1[:], 256)
+        ql0 = quant("hql0", hl0[:], 256)
+        head(768, 256, q10, 256, ql1, "sssv", [4, 5, 6, 7])
+        head(512, 256, q10, 0, ql0, "svsv", [4, 5, 6, 7])
+        head(0, 512, q00, 0, q01, "ssss", [0, 1, 2, 3])

@@ -45,67 +45,70 @@ def tile_list_patch_maxout_evidence_kernel(tc, tab_words, tab_scales, offs, w1, 
         offs_t = first.tile([P, S // 16], U16, name="offs_t")
         nc.sync.dma_start(offs_t[:], offs)
 
-        rows_raw = first.tile([4, PASS], F32, name="rows_raw", align_bytes=64)
+        rows_raw = first.tile([4, PASS], F32, name="rows_raw", tag="rows_raw", align_bytes=64)
         nc.sync.dma_start(out=rows_raw[0:2, :], in_=b1.rearrange("(b c) -> b c", b=2))
         nc.sync.dma_start(out=rows_raw[2:4, :], in_=b2.rearrange("(b c) -> b c", b=2))
-
-        tsc = first.tile([P, 2, T // 4], I32, name="tsc", align_bytes=64)
-        w2s_raw = first.tile([P, 2, H // 4], I32, name="w2s_raw", tag="w2s_raw", align_bytes=64)
-        rows = first.tile([P, PASS], F32, name="rows", align_bytes=64)
-        rows_c = first.tile([P, P], F32, name="rows_c", align_bytes=64)
+        tsc = first.tile([P, T // 4], I32, name="tsc", tag="tsc", align_bytes=64)
         ident = first.tile([P, P], F32, name="ident", align_bytes=64)
-        nc.gpsimd.memset(tsc[:, 0, :], 0)
-        nc.vector.memset(tsc[:, 1, :], 0)
-        nc.vector.memset(w2s_raw[:], 0)
+        nc.vector.memset(tsc[:], 0)
         with tc.tile_pool(name="setup", bufs=1) as setup:
             diag = setup.tile([P, P], I32, name="diag")
             nc.gpsimd.iota(diag[:], pattern=[[-1, P]], base=0, channel_multiplier=1)
             nc.vector.tensor_scalar(out=ident[:], in0=diag[:], scalar1=0.0, scalar2=None, op0=IS_EQUAL)
-        nc.vector.memset(rows[:], 0.0)
-        nc.vector.memset(rows_c[:], 0.0)
         held = ctx.enter_context(tc.tile_pool(name="held", bufs=1))
 
         def place(shape, dtype, name, size, over):
-            pool = first if over == "w2s_raw" else held
+            pool = first if over in ("tsc", "rows_raw") else held
             return pool.tile(shape, dtype, name=name, tag=over or name, align_bytes=64)
 
-        tsc_src = tab_scales.bitcast(I32).rearrange("a (q r) n -> r q a n", r=4)
-        for r in range(4):
-            nc.sync.dma_start(out=tsc[r:P:32, :, :], in_=tsc_src[r])
+        w2s_raw = place([P, 2, H // 4], I32, "w2s_raw", 0, None)
+        rows = place([P, PASS], F32, "rows", 0, None)
+        rows_c = place([P, P], F32, "rows_c", 0, None)
+        gs1 = place([P, S // 4], I32, "gs1", 0, None)
+        gsp = place([P, S], U8, "gsp", 0, None)
+        nc.vector.memset(w2s_raw[:], 0)
+        nc.vector.memset(rows[:], 0.0)
+        nc.vector.memset(gs1[:], 0)
+        nc.vector.memset(rows_c[:], 0.0)
         w2s_src = w2_scales.bitcast(I32).rearrange("a (q r) n -> r q a n", r=4)
-        tw = [place([P, T], I32, "tw%d" % a, 0, None) for a in range(2)]
-        w2w_raw = place([P, 2, H // 2], I32, "w2w_raw", 0, "w2w_raw")
+        for q in range(4):
+            nc.sync.dma_start(out=tsc[32 * q:32 * q + 8, :], in_=tab_scales.bitcast(I32)[:, 4 * q:4 * q + 4, :])
+        tw = [place([P, T], I32, "tw0", 0, None)]
+        w2w_raw = place([P, 2, H // 2], I32, "w2w_raw", 0, None)
+        nc.sync.dma_start(out=tw[0][:], in_=tab_words[0].rearrange("p t i -> p (t i)").bitcast(I32))
+        nc.sync.dma_start(out=w2w_raw[:], in_=w2_words.bitcast(I32).rearrange("a p n -> p a n"))
+        for r in range(4):
+            nc.sync.dma_start(out=w2s_raw[r:P:32, :, :], in_=w2s_src[r])
+        nc.scalar.copy(
+            out=rows[0:4, :].rearrange("b (t g i) -> b t g i", t=4, i=4),
+            in_=rows_raw[:].rearrange("b (g t i) -> b t g i", t=4, i=4),
+        )
+        tw.append(place([P, T], I32, "tw1", 0, "rows_raw"))
+        nc.sync.dma_start(out=tw[1][:], in_=tab_words[1].rearrange("p t i -> p (t i)").bitcast(I32))
+        nc.vector.tensor_copy(out=gsp[:], in_=tsc[:].bitcast(U8).indirect(offs_t[:]))
+        for r in range(4):
+            nc.sync.dma_start(out=gs1[r:P:32, :], in_=gsp[:].bitcast(I32)[4 + r:P:32, :])
+
         w1_raw = {}
         wc_raw = {}
 
-        def load_w1(a, b):
-            t_w = place([P, 4, PASS], F32, "w1raw%d%d" % (a, b), 0, "w%d%d" % (a, b))
+        def load_w1(a, b, over):
+            t_w = place([P, 4, PASS], F32, "w1raw%d%d" % (a, b), 0, over)
             nc.sync.dma_start(
                 out=t_w[:],
                 in_=w1[a * PASS:(a + 1) * PASS, b * PASS:(b + 1) * PASS].rearrange("(p j) c -> p j c", j=4),
             )
             w1_raw[a, b] = t_w
 
-        def load_wc(b):
-            t_w = place([P, 4, N], F32, "wcraw%d" % b, 0, "wc%d" % b)
+        def load_wc(b, over):
+            t_w = place([P, 4, N], F32, "wcraw%d" % b, 0, over)
             src = wc[b * PASS:(b + 1) * PASS, :].rearrange("(g t i) n -> t g i n", t=4, i=4)
             for t in range(4):
                 nc.sync.dma_start(out=t_w[:, t, :], in_=src[t])
             wc_raw[b] = t_w
 
-        nc.sync.dma_start(out=tw[0][:], in_=tab_words[0].rearrange("p t i -> p (t i)").bitcast(I32))
-        nc.sync.dma_start(out=w2w_raw[:], in_=w2_words.bitcast(I32).rearrange("a p n -> p a n"))
-        for r in range(4):
-            nc.sync.dma_start(out=w2s_raw[r:P:32, :, :], in_=w2s_src[r])
-        nc.sync.dma_start(out=tw[1][:], in_=tab_words[1].rearrange("p t i -> p (t i)").bitcast(I32))
-        load_w1(1, 0)
-        load_w1(0, 0)
-        load_w1(0, 1)
-        load_w1(1, 1)
-        load_wc(1)
-        load_wc(0)
-
         nc.sync.dma_start(out=rows_c[0:4, :], in_=bc.rearrange("(m p) -> m p", p=P))
+        load_w1(1, 0, "tsc")
         bias_c = first.tile([P, 4], F32, name="bias_c")
 
         def make_bias_c(k):
@@ -117,11 +120,11 @@ def tile_list_patch_maxout_evidence_kernel(tc, tab_words, tab_scales, offs, w1, 
         gs = {}
         gs_b = {}
 
-        def gather_scales(a, c, over=None):
-            g = place([P, HALF], U8, "gs%d%d" % (a, c), 512, over)
-            nc.vector.tensor_copy(out=g[:], in_=tsc[:, a, :].bitcast(U8).indirect(offs_t[:, 32 * c:32 * (c + 1)]))
-            gs[a, c] = g[:]
-            gs_b[a, c] = g[:]
+        for c in range(2):
+            gs[0, c] = gsp[:, c * HALF:(c + 1) * HALF]
+            gs[1, c] = gsp[4:P, c * HALF:(c + 1) * HALF]
+            gs_b[0, c] = gs[0, c]
+            gs_b[1, c] = gs1[:].bitcast(U8)[:, c * HALF:(c + 1) * HALF]
 
         def gather_words(a, c, over=None):
             g = place([P, HALF], U32, "gw%d%d" % (a, c), 2048, over)
@@ -144,10 +147,6 @@ def tile_list_patch_maxout_evidence_kernel(tc, tab_words, tab_scales, offs, w1, 
         bias = first.tile([P, 4, 4], F32, name="bias")
 
         def make_bias():
-            nc.scalar.copy(
-                out=rows[0:4, :].rearrange("b (t g i) -> b t g i", t=4, i=4),
-                in_=rows_raw[:].rearrange("b (g t i) -> b t g i", t=4, i=4),
-            )
             bias_ps = bank(7, [P, 4, P])
             for t in range(4):
                 nc.tensor.transpose(bias_ps[:, t, :], rows[:, t * P:(t + 1) * P], ident[:])
@@ -256,59 +255,60 @@ def tile_list_patch_maxout_evidence_kernel(tc, tab_words, tab_scales, offs, w1, 
         make_bias()
         w1bf = [place([P, 2, 4 * PASS], BF16, "w1bf%d" % b, 0, None) for b in range(2)]
         wcbf = place([P, 2, 4 * N], BF16, "wcbf", 0, None)
-        gather_scales(0, 0)
-        gather_scales(1, 0)
         gather_words(0, 0)
         order_w2()
-        gather_scales(0, 1, "w2s_raw")
+        load_w1(0, 0, "w2w_raw")
         gather_words(1, 0)
         branch_b(0, 0, 0)
         branch_b(0, 1, 4)
-        gather_scales(1, 1, "w2w_raw")
+        gather_words(0, 1, "w2s_raw")
+        load_w1(0, 1, "tw0")
         gather_words(1, 1)
-        gather_words(0, 1, "tw1")
-        cast_w1(0, 1, "v", w1bf[1][:, 0, :])
+        load_w1(1, 1, "rows_raw")
         cast_w1(1, 0, "v", w1bf[0][:, 1, :])
-        branch_b(1, 0, 0)
+        load_wc(1, "tsc")
         cast_w1(0, 0, "v", w1bf[0][:, 0, :])
+        load_wc(0, "w2w_raw")
+        interleave("s", wcbf[:, 0, :], wc_raw[0][:])
+        cast_w1(1, 1, "s", w1bf[1][:, 1, :])
+        cast_w1(0, 1, "v", w1bf[1][:, 0, :])
         cq, cs = quant("w1q0", w1bf[0][:].rearrange("p a n -> p (a n)"), 2 * PASS)
         for a in range(2):
             w1q[a, 0] = (cq[:, a * PASS:(a + 1) * PASS], cs[:, a * PASS:(a + 1) * PASS])
-        cast_w1(1, 1, "s", w1bf[1][:, 1, :])
-        a00 = branch_a(0, 0, 0)
+        branch_b(1, 0, 0)
         interleave("v", wcbf[:, 1, :], wc_raw[1][:])
-        p00 = maxout(a00, 0, 0, 0, 512)
-        cq, cs = quant("w1q1", w1bf[1][:].rearrange("p a n -> p (a n)"), 2 * PASS, "w00")
+        a00 = branch_a(0, 0, 4)
+        cq, cs = quant("w1q1", w1bf[1][:].rearrange("p a n -> p (a n)"), 2 * PASS)
         for a in range(2):
             w1q[a, 1] = (cq[:, a * PASS:(a + 1) * PASS], cs[:, a * PASS:(a + 1) * PASS])
-        branch_b(1, 1, 4, "bb00")
+        p00 = maxout(a00, 0, 0, 0, 512)
         a01 = branch_a(0, 1, 0)
-        p01 = maxout(a01, 0, 1, 0, 512)
-        a10 = branch_a(1, 0, 4)
+        branch_b(1, 1, 4, "bb00")
         h00 = place([P, 2048], BF16, "h00", 0, None)
         interleave("s", h00[:], p00)
-        q00 = quant("hq00", h00[:], 512, "wc1")
-        p10 = maxout(a10, 1, 0, 0, 512)
-        make_bias_c(3)
-        h10 = place([P, 2048], BF16, "h10", 0, "w10")
-        interleave("s", h10[:], p10)
-        a11 = branch_a(1, 1, 4)
-        interleave("s", wcbf[:, 0, :], wc_raw[0][:])
-        q10 = quant("hq10", h10[:], 512, "bb10")
+        p01 = maxout(a01, 0, 1, 0, 512, "w1bf1")
+        q00 = quant("hq00", h00[:], 512)
+        a10 = branch_a(1, 0, 4)
+        h01 = place([P, 2048], BF16, "h01", 0, None)
+        interleave("s", h01[:], p01)
         cq, cs = quant("wcq", wcbf[:].rearrange("p b n -> p (b n)"), 2 * N)
         for b in range(2):
             wcq[b] = (cq[:, b * N:(b + 1) * N], cs[:, b * N:(b + 1) * N])
+        p10 = maxout(a10, 1, 0, 0, 512)
+        make_bias_c(4)
+        h10 = place([P, 2048], BF16, "h10", 0, None)
+        interleave("s", h10[:], p10)
+        a11 = branch_a(1, 1, 4)
         pl1 = maxout(a11, 1, 1, 256, 256)
-        h01 = place([P, 2048], BF16, "h01", 0, None)
-        interleave("s", h01[:], p01)
         hl1 = place([P, 1024], BF16, "hl1", 0, None)
         interleave("v", hl1[:], pl1)
+        q10 = quant("hq10", h10[:], 512)
+        pl0 = maxout(a11, 1, 1, 0, 256)
         q01 = quant("hq01", h01[:], 512)
-        pl0 = maxout(a11, 1, 1, 0, 256, "planes000")
         hl0 = place([P, 1024], BF16, "hl0", 0, None)
         interleave("v", hl0[:], pl0)
         ql1 = quant("hql1", hl1[:], 256)
-        ql0 = quant("hql0", hl0[:], 256)
         head(768, 256, q10, 256, ql1, "sssv", [4, 5, 6, 7])
-        head(512, 256, q10, 0, ql0, "svsv", [4, 5, 6, 7])
+        ql0 = quant("hql0", hl0[:], 256)
         head(0, 512, q00, 0, q01, "ssss", [0, 1, 2, 3])
+        head(512, 256, q10, 0, ql0, "svss", [0, 1, 2, 3])

@@ -265,50 +265,55 @@ def tile_list_patch_maxout_evidence_kernel(tc, tab_words, tab_scales, offs, w1, 
         load_w1(0, 1, "tw0")
         gather_words(1, 1)
         load_w1(1, 1, "rows_raw")
-        cast_w1(1, 0, "v", w1bf[0][:, 1, :])
-        load_wc(1, "tsc")
         cast_w1(0, 0, "v", w1bf[0][:, 0, :])
         load_wc(0, "w2w_raw")
         interleave("s", wcbf[:, 0, :], wc_raw[0][:])
-        cast_w1(1, 1, "s", w1bf[1][:, 1, :])
         cast_w1(0, 1, "v", w1bf[1][:, 0, :])
+        cast_w1(1, 0, "v", w1bf[0][:, 1, :])
+        load_wc(1, "tsc")
         cq, cs = quant("w1q0", w1bf[0][:].rearrange("p a n -> p (a n)"), 2 * PASS)
         for a in range(2):
             w1q[a, 0] = (cq[:, a * PASS:(a + 1) * PASS], cs[:, a * PASS:(a + 1) * PASS])
-        branch_b(1, 0, 0)
-        interleave("v", wcbf[:, 1, :], wc_raw[1][:])
+        branch_b(1, 0, 4)
+        cast_w1(1, 1, "s", w1bf[1][:, 1, :])
+        make_bias_c(0)
         a00 = branch_a(0, 0, 4)
         cq, cs = quant("w1q1", w1bf[1][:].rearrange("p a n -> p (a n)"), 2 * PASS)
         for a in range(2):
             w1q[a, 1] = (cq[:, a * PASS:(a + 1) * PASS], cs[:, a * PASS:(a + 1) * PASS])
         p00 = maxout(a00, 0, 0, 0, 512)
-        a01 = branch_a(0, 1, 0)
-        branch_b(1, 1, 4, "bb00")
+        branch_b(1, 1, 4, "rows_raw")
         h00 = place([P, 2048], BF16, "h00", 0, None)
-        interleave("s", h00[:], p00)
-        p01 = maxout(a01, 0, 1, 0, 512, "w1bf1")
-        q00 = quant("hq00", h00[:], 512)
-        a10 = branch_a(1, 0, 4)
+        interleave("v", h00[:], p00)
+        a01 = branch_a(0, 1, 0)
+        p01 = maxout(a01, 0, 1, 0, 512)
+        a10 = branch_a(1, 0, 0)
         h01 = place([P, 2048], BF16, "h01", 0, None)
         interleave("s", h01[:], p01)
+        a11 = branch_a(1, 1, 4)
+        p10 = maxout(a10, 1, 0, 0, 512)
+        q01 = quant("hq01", h01[:], 512)
+        h10 = place([P, 2048], BF16, "h10", 0, None)
+        interleave("s", h10[:], p10)
+        interleave("v", wcbf[:, 1, :], wc_raw[1][:])
         cq, cs = quant("wcq", wcbf[:].rearrange("p b n -> p (b n)"), 2 * N)
         for b in range(2):
             wcq[b] = (cq[:, b * N:(b + 1) * N], cs[:, b * N:(b + 1) * N])
-        p10 = maxout(a10, 1, 0, 0, 512)
-        make_bias_c(4)
-        h10 = place([P, 2048], BF16, "h10", 0, None)
-        interleave("s", h10[:], p10)
-        a11 = branch_a(1, 1, 4)
-        pl1 = maxout(a11, 1, 1, 256, 256)
-        hl1 = place([P, 1024], BF16, "hl1", 0, None)
-        interleave("v", hl1[:], pl1)
-        q10 = quant("hq10", h10[:], 512)
+        q00 = quant("hq00", h00[:], 512, "w1bf1")
         pl0 = maxout(a11, 1, 1, 0, 256)
-        q01 = quant("hq01", h01[:], 512)
         hl0 = place([P, 1024], BF16, "hl0", 0, None)
         interleave("v", hl0[:], pl0)
-        ql1 = quant("hql1", hl1[:], 256)
-        head(768, 256, q10, 256, ql1, "sssv", [4, 5, 6, 7])
-        ql0 = quant("hql0", hl0[:], 256)
         head(0, 512, q00, 0, q01, "ssss", [0, 1, 2, 3])
-        head(512, 256, q10, 0, ql0, "svss", [0, 1, 2, 3])
+        ql0 = quant("hql0", hl0[:], 256)
+        q10 = quant("hq10", h10[:], 512, "bb01")
+        pl1 = maxout(a11, 1, 1, 256, 128)
+        hl1 = place([P, 512], BF16, "hl1", 0, None)
+        interleave("v", hl1[:], pl1)
+        pl2 = maxout(a11, 1, 1, 384, 128)
+        ql1 = quant("hql1", hl1[:], 128)
+        hl2 = place([P, 512], BF16, "hl2", 0, None)
+        interleave("v", hl2[:], pl2)
+        head(512, 256, q10, 0, ql0, "ssss", [0, 1, 2, 3])
+        ql2 = quant("hql2", hl2[:], 128)
+        head(768, 128, q10, 256, ql1, "svsv", [4, 5, 6, 7])
+        head(896, 128, q10, 384, ql2, "svss", [0, 1, 2, 3])

from contextlib import ExitStack

import concourse.mybir as mybir

K, H, N, T, S = 1024, 1024, 512, 2048, 1024
FLOPS = 2 * S * (2 * K * H + H * N)

F32 = mybir.dt.float32
BF16 = mybir.dt.bfloat16
I32 = mybir.dt.int32
U32 = mybir.dt.uint32
U16 = mybir.dt.uint16
U8 = mybir.dt.uint8
FP8X4 = mybir.dt.float8_e4m3fn_x4
FP4X4 = mybir.dt.float4_e2m1fn_x4
ADD = mybir.AluOpType.add
MULT = mybir.AluOpType.mult
MAX = mybir.AluOpType.max
IS_EQUAL = mybir.AluOpType.is_equal
IDENT = mybir.ActivationFunctionType.Identity

P = 128
PASS = 512
HALF = 512


def move(nc, eng, out, in_):
    if eng == "v":
        nc.vector.tensor_copy(out=out, in_=in_)
    elif eng == "s":
        nc.scalar.copy(out=out, in_=in_)
    else:
        nc.gpsimd.tensor_scalar(out=out, in0=in_, scalar1=1.0, scalar2=0.0, op0=MULT, op1=ADD)


def tile_list_patch_maxout_evidence_kernel(tc, tab_words, tab_scales, offs, w1, b1, w2_words, w2_scales, b2, wc, bc, out):
    nc = tc.nc
    with ExitStack() as ctx:
        first = ctx.enter_context(tc.tile_pool(name="first", bufs=1))
        psum = ctx.enter_context(tc.psum_pool(name="psum", bufs=1))

        def bank(k, shape):
            return psum.tile(shape, F32, name="bank%d" % k, tag="bank%d" % k)

        offs_t = first.tile([P, S // 16], U16, name="offs_t")
        nc.sync.dma_start(offs_t[:], offs)

        rows_raw = first.tile([4, PASS], F32, name="rows_raw", tag="rows_raw", align_bytes=64)
        nc.sync.dma_start(out=rows_raw[0:2, :], in_=b1.rearrange("(b c) -> b c", b=2))
        nc.sync.dma_start(out=rows_raw[2:4, :], in_=b2.rearrange("(b c) -> b c", b=2))
        tsc = first.tile([P, T // 4], I32, name="tsc", tag="tsc", align_bytes=64)
        ident = first.tile([P, P], F32, name="ident", align_bytes=64)
        nc.vector.memset(tsc[:], 0)
        with tc.tile_pool(name="setup", bufs=1) as setup:
            diag = setup.tile([P, P], I32, name="diag")
            nc.gpsimd.iota(diag[:], pattern=[[-1, P]], base=0, channel_multiplier=1)
            nc.vector.tensor_scalar(out=ident[:], in0=diag[:], scalar1=0.0, scalar2=None, op0=IS_EQUAL)
        held = ctx.enter_context(tc.tile_pool(name="held", bufs=1))

        def place(shape, dtype, name, size, over):
            pool = first if over in ("tsc", "rows_raw") else held
            return pool.tile(shape, dtype, name=name, tag=over or name, align_bytes=64)

        w2s_raw = place([P, 2, H // 4], I32, "w2s_raw", 0, None)
        rows = place([P, PASS], F32, "rows", 0, None)
        rows_c = place([P, P], F32, "rows_c", 0, None)
        gs1 = place([P, S // 4], I32, "gs1", 0, None)
        gsp = place([P, S], U8, "gsp", 0, None)
        nc.vector.memset(w2s_raw[:], 0)
        nc.vector.memset(rows[:], 0.0)
        nc.vector.memset(gs1[:], 0)
        nc.vector.memset(rows_c[:], 0.0)
        w2s_src = w2_scales.bitcast(I32).rearrange("a (q r) n -> r q a n", r=4)
        for q in range(4):
            nc.sync.dma_start(out=tsc[32 * q:32 * q + 8, :], in_=tab_scales.bitcast(I32)[:, 4 * q:4 * q + 4, :])
        tw = [place([P, T], I32, "tw0", 0, None)]
        w2w_raw = place([P, 2, H // 2], I32, "w2w_raw", 0, None)
        nc.sync.dma_start(out=tw[0][:], in_=tab_words[0].rearrange("p t i -> p (t i)").bitcast(I32))
        nc.sync.dma_start(out=w2w_raw[:], in_=w2_words.bitcast(I32).rearrange("a p n -> p a n"))
        for r in range(4):
            nc.sync.dma_start(out=w2s_raw[r:P:32, :, :], in_=w2s_src[r])
        nc.scalar.copy(
            out=rows[0:4, :].rearrange("b (t g i) -> b t g i", t=4, i=4),
            in_=rows_raw[:].rearrange("b (g t i) -> b t g i", t=4, i=4),
        )
        tw.append(place([P, T], I32, "tw1", 0, "rows_raw"))
        nc.sync.dma_start(out=tw[1][:], in_=tab_words[1].rearrange("p t i -> p (t i)").bitcast(I32))
        nc.vector.tensor_copy(out=gsp[:], in_=tsc[:].bitcast(U8).indirect(offs_t[:]))
        for r in range(4):
            nc.sync.dma_start(out=gs1[r:P:32, :], in_=gsp[:].bitcast(I32)[4 + r:P:32, :])

        w1_raw = {}
        wc_raw = {}

        def load_w1(a, b, over):
            t_w = place([P, 4, PASS], F32, "w1raw%d%d" % (a, b), 0, over)
            nc.sync.dma_start(
                out=t_w[:],
                in_=w1[a * PASS:(a + 1) * PASS, b * PASS:(b + 1) * PASS].rearrange("(p j) c -> p j c", j=4),
            )
            w1_raw[a, b] = t_w

        def load_wc(b, over):
            t_w = place([P, 4, N], F32, "wcraw%d" % b, 0, over)
            src = wc[b * PASS:(b + 1) * PASS, :].rearrange("(g t i) n -> t g i n", t=4, i=4)
            for t in range(4):
                nc.sync.dma_start(out=t_w[:, t, :], in_=src[t])
            wc_raw[b] = t_w

        nc.sync.dma_start(out=rows_c[0:4, :], in_=bc.rearrange("(m p) -> m p", p=P))
        load_w1(1, 0, "tsc")
        bias_c = first.tile([P, 4], F32, name="bias_c")

        def make_bias_c(k):
            bias_c_ps = bank(k, [P, P])
            nc.tensor.transpose(bias_c_ps[:], rows_c[:], ident[:])
            nc.scalar.activation(out=bias_c[:], in_=bias_c_ps[:, 0:4], func=IDENT)

        gw = {}
        gs = {}
        gs_b = {}

        for c in range(2):
            gs[0, c] = gsp[:, c * HALF:(c + 1) * HALF]
            gs[1, c] = gsp[4:P, c * HALF:(c + 1) * HALF]
            gs_b[0, c] = gs[0, c]
            gs_b[1, c] = gs1[:].bitcast(U8)[:, c * HALF:(c + 1) * HALF]

        def gather_words(a, c, over=None):
            g = place([P, HALF], U32, "gw%d%d" % (a, c), 2048, over)
            nc.vector.tensor_copy(out=g[:], in_=tw[a][:].bitcast(U32).indirect(offs_t[:, 32 * c:32 * (c + 1)]))
            gw[a, c] = g

        w2w = held.tile([P, 4, 4, 64], I32, name="w2w", align_bytes=64)
        w2s = held.tile([P, 4, 4, 32], I32, name="w2s", align_bytes=64)

        def order_w2():
            nc.vector.tensor_copy(
                out=w2w[:].rearrange("p u t (g w) -> p u t g w", w=2),
                in_=w2w_raw[:].rearrange("p a (b g t w) -> p (a b) t g w", b=2, t=4, w=2),
            )
            nc.vector.tensor_copy(
                out=w2s[:].rearrange("p u t g -> p u g t"),
                in_=w2s_raw[:].rearrange("p a (b g t) -> p (a b) g t", b=2, t=4),
            )

        bias = first.tile([P, 4, 4], F32, name="bias")

        def make_bias():
            bias_ps = bank(7, [P, 4, P])
            for t in range(4):
                nc.tensor.transpose(bias_ps[:, t, :], rows[:, t * P:(t + 1) * P], ident[:])
            nc.scalar.activation(out=bias[:], in_=bias_ps[:, :, 0:4], func=IDENT)

        bb = {}

        def branch_b(c, b, k0, over=None):
            accs = [bank(k0 + t, [P, HALF]) for t in range(4)]
            for a in range(2):
                for t in range(4):
                    nc.tensor.matmul_mx(
                        out=accs[t][:],
                        lhsT=w2w[:, 2 * a + b, t, :].bitcast(U8).bitcast(FP4X4),
                        lhsT_scale=w2s[:, 2 * a + b, t, :].bitcast(U8),
                        rhs=gw[a, c][:].bitcast(FP8X4),
                        rhs_scale=gs_b[a, c],
                        start=(a == 0),
                        stop=(a == 1),
                    )
            v = place([P, 4, HALF], F32, "bb%d%d" % (c, b), 0, over)
            for t in range(4):
                nc.scalar.activation(out=v[:, t, :], in_=accs[t][:], func=IDENT, bias=bias[:, t, 2 + b:3 + b])
                bb[c, b, t] = v[:, t, :]

        def cast_w1(a, b, eng, g):
            dst = g.rearrange("p (t g i j) -> p t g j i", t=4, i=4, j=4)
            src = w1_raw[a, b][:].rearrange("p j (g t i) -> p t g j i", t=4, i=4)
            if eng == "g":
                for t in range(4):
                    move(nc, eng, dst[:, t], src[:, t])
            else:
                move(nc, eng, dst, src)

        def quant(name, g, width, over=None):
            codes = place([P, width], U32, name + "c", 4 * width, over)
            scales = held.tile([P, width], U8, name=name + "s", align_bytes=64)
            nc.vector.quantize_mx(out=codes[:].bitcast(FP8X4), scales=scales[:], in_=g)
            return codes, scales

        def interleave(eng, g, raw):
            dst = g.rearrange("p (c i t) -> p c t i", i=4, t=4)
            src = raw.rearrange("p t (c i) -> p c t i", i=4)
            parts = 4 if eng == "g" else 1
            w = dst.shape[1] // parts
            for u in range(parts):
                move(nc, eng, dst[:, u * w:(u + 1) * w], src[:, u * w:(u + 1) * w])

        w1q = {}
        wcq = {}

        def branch_a(c, b, k0):
            accs = [bank(k0 + t, [P, HALF]) for t in range(4)]
            for t in range(4):
                for a in range(2):
                    codes, scales = w1q[a, b]
                    nc.tensor.matmul_mx(
                        out=accs[t][:],
                        lhsT=codes[:, t * P:(t + 1) * P].bitcast(FP8X4),
                        lhsT_scale=scales[:, t * P:(t + 1) * P],
                        rhs=gw[a, c][:].bitcast(FP8X4),
                        rhs_scale=gs[a, c],
                        start=(a == 0),
                        stop=(a == 1),
                    )
            return accs

        def maxout(accs, c, b, lo, width, over=None):
            planes = place([P, 4, width], BF16, "planes%d%d%d" % (c, b, lo), 8 * width, over)
            for t in range(4):
                nc.vector.scalar_tensor_tensor(
                    out=planes[:, t, :], in0=accs[t][:, lo:lo + width], scalar=bias[:, t, b:b + 1],
                    in1=bb[c, b, t][:, lo:lo + width], op0=ADD, op1=MAX,
                )
            return planes[:]

        def head(col, width, h0, lo0, h1, engs, banks):
            per = 4 // len(banks)
            tiles = [bank(k, [P, per, width]) for k in banks]
            accs = [tiles[m // per][:, m % per, :] for m in range(4)]
            order = [(b, m) for b in range(2) for m in range(4)] if per == 1 else [(b, m) for m in range(4) for b in range(2)]
            for b, m in order:
                codes, scales = wcq[b]
                hc, hs = (h0, h1)[b]
                lo = lo0 if b == 0 else 0
                nc.tensor.matmul_mx(
                    out=accs[m],
                    lhsT=codes[:, m * P:(m + 1) * P].bitcast(FP8X4),
                    lhsT_scale=scales[:, m * P:(m + 1) * P],
                    rhs=hc[:, lo:lo + width].bitcast(FP8X4),
                    rhs_scale=hs[:, lo:lo + width],
                    start=(b == 0),
                    stop=(b == 1),
                )
            dst = out.rearrange("(m p) n -> p m n", p=P)
            per_store = 1 if width == HALF else 2
            for m0 in range(0, 4, per_store):
                res = held.tile([P, per_store, width], F32, name="res%d_%d" % (col, m0))
                for m in range(m0, m0 + per_store):
                    if engs[m] == "s":
                        nc.scalar.activation(out=res[:, m - m0, :], in_=accs[m], func=IDENT, bias=bias_c[:, m:m + 1])
                    else:
                        nc.vector.tensor_scalar(out=res[:, m - m0, :], in0=accs[m], scalar1=bias_c[:, m:m + 1], scalar2=None, op0=ADD)
                nc.sync.dma_start(out=dst[:, m0:m0 + per_store, col:col + width], in_=res[:])

        make_bias()
        w1bf = [place([P, 2, 4 * PASS], BF16, "w1bf%d" % b, 0, None) for b in range(2)]
        wcbf = place([P, 2, 4 * N], BF16, "wcbf", 0, None)
        gather_words(0, 0)
        order_w2()
        load_w1(0, 0, "w2w_raw")
        gather_words(1, 0)
        branch_b(0, 0, 0)
        branch_b(0, 1, 4)
        gather_words(0, 1, "w2s_raw")
        load_w1(0, 1, "tw0")
        gather_words(1, 1)
        load_w1(1, 1, "rows_raw")
        cast_w1(0, 0, "v", w1bf[0][:, 0, :])
        load_wc(0, "w2w_raw")
        interleave("s", wcbf[:, 0, :], wc_raw[0][:])
        cast_w1(0, 1, "v", w1bf[1][:, 0, :])
        cast_w1(1, 0, "v", w1bf[0][:, 1, :])
        load_wc(1, "tsc")
        cq, cs = quant("w1q0", w1bf[0][:].rearrange("p a n -> p (a n)"), 2 * PASS)
        for a in range(2):
            w1q[a, 0] = (cq[:, a * PASS:(a + 1) * PASS], cs[:, a * PASS:(a + 1) * PASS])
        branch_b(1, 0, 4)
        cast_w1(1, 1, "s", w1bf[1][:, 1, :])
        make_bias_c(0)
        a00 = branch_a(0, 0, 4)
        cq, cs = quant("w1q1", w1bf[1][:].rearrange("p a n -> p (a n)"), 2 * PASS)
        for a in range(2):
            w1q[a, 1] = (cq[:, a * PASS:(a + 1) * PASS], cs[:, a * PASS:(a + 1) * PASS])
        p00 = maxout(a00, 0, 0, 0, 512)
        branch_b(1, 1, 4, "rows_raw")
        h00 = place([P, 2048], BF16, "h00", 0, None)
        interleave("v", h00[:], p00)
        a01 = branch_a(0, 1, 0)
        p01 = maxout(a01, 0, 1, 0, 512)
        a10 = branch_a(1, 0, 0)
        h01 = place([P, 2048], BF16, "h01", 0, None)
        interleave("s", h01[:], p01)
        a11 = branch_a(1, 1, 4)
        p10 = maxout(a10, 1, 0, 0, 512)
        q01 = quant("hq01", h01[:], 512)
        h10 = place([P, 2048], BF16, "h10", 0, None)
        interleave("s", h10[:], p10)
        interleave("v", wcbf[:, 1, :], wc_raw[1][:])
        cq, cs = quant("wcq", wcbf[:].rearrange("p b n -> p (b n)"), 2 * N)
        for b in range(2):
            wcq[b] = (cq[:, b * N:(b + 1) * N], cs[:, b * N:(b + 1) * N])
        q00 = quant("hq00", h00[:], 512, "w1bf1")
        pl0 = maxout(a11, 1, 1, 0, 256)
        hl0 = place([P, 1024], BF16, "hl0", 0, None)
        interleave("v", hl0[:], pl0)
        head(0, 512, q00, 0, q01, "ssss", [0, 1, 2, 3])
        ql0 = quant("hql0", hl0[:], 256)
        q10 = quant("hq10", h10[:], 512, "bb01")
        pl1 = maxout(a11, 1, 1, 256, 128)
        hl1 = place([P, 512], BF16, "hl1", 0, None)
        interleave("v", hl1[:], pl1)
        pl2 = maxout(a11, 1, 1, 384, 128)
        ql1 = quant("hql1", hl1[:], 128)
        hl2 = place([P, 512], BF16, "hl2", 0, None)
        interleave("v", hl2[:], pl2)
        head(512, 256, q10, 0, ql0, "ssss", [0, 1, 2, 3])
        ql2 = quant("hql2", hl2[:], 128)
        head(768, 128, q10, 256, ql1, "svsv", [4, 5, 6, 7])
        head(896, 128, q10, 384, ql2, "svss", [0, 1, 2, 3])
